import numpy as np
import ml_dtypes


def mxq(x, axis, fmt="e4m3"):
    dtype, down = {"e4m3": (ml_dtypes.float8_e4m3fn, 7), "e5m2": (ml_dtypes.float8_e5m2, 14)}[fmt]
    v = np.moveaxis(np.asarray(x, np.float32).astype(ml_dtypes.bfloat16).astype(np.float64), axis, -1)
    blocks = v.reshape(v.shape[:-1] + (-1, 32))
    amax = np.abs(blocks).max(-1, keepdims=True)
    byte = np.maximum(np.where(amax > 0, np.frexp(amax)[1] - 1 + 127, 0) - down, 1)
    scale = np.exp2(byte - 127.0)
    codes = (blocks / scale).astype(np.float32).astype(dtype).astype(np.float64)
    return np.moveaxis((codes * scale).reshape(v.shape), -1, axis)


WIDE = False


def mx_kscale(k):
    if not WIDE:
        return np.ones(k)
    levels = np.array([10, -10, 5, -5, 0])
    if k % 512:
        return np.exp2(np.random.permutation(np.resize(levels, k // 32))).repeat(32)
    a = np.empty((k // 512, 16))
    for p in range(k // 512):
        a[p, :8] = np.random.permutation(np.resize(levels, 8))
        for g in range(8):
            far = levels[np.abs(levels - a[p, g]) >= 10]
            a[p, g + 8] = far[np.random.randint(len(far))]
    return np.exp2(a.ravel()).repeat(32)


def f64(x):
    return np.asarray(x).astype(np.float64)


def striped(idx):
    return np.tile(idx.reshape(-1, 16).T, (8, 1)).astype(np.uint16)


def unstriped(offs):
    return offs[:16].T.reshape(-1).astype(np.int64)


def pack_weight(w):
    k, n = w.shape
    w = f64(np.asarray(w, np.float32).astype(ml_dtypes.bfloat16)).reshape(k // 32, 32, n)
    amax = np.abs(w).max(1)
    byte = np.clip(np.where(amax > 0, np.frexp(amax)[1] - 1 + 127 - 7, 1), 1, 254)
    scaled = (w * np.exp2(127.0 - byte)[:, None, :]).reshape(k, n).astype(np.float32)
    words = np.ascontiguousarray(scaled.reshape(k // 512, 128, 4, n).transpose(0, 1, 3, 2)).astype(ml_dtypes.float8_e4m3fn).view(np.uint8)
    return words, np.ascontiguousarray(byte.astype(np.uint8).reshape(k // 512, 16, n))


def unpack_weight(words, scales):
    g, p, n, _ = words.shape
    vals = np.ascontiguousarray(words).view(ml_dtypes.float8_e4m3fn).astype(np.float64) * np.repeat(np.exp2(scales.astype(np.float64) - 127.0), 8, axis=1)[..., None]
    return vals.transpose(0, 1, 3, 2).reshape(g * 512, n)


K, T, S, D, N, H, V, U = 512, 4096, 1024, 4, 128, 512, 256, 512


def setup_inputs():
    n = np.random.standard_normal
    s = mx_kscale(K)[:, None]
    u = mx_kscale(H)
    packed_xT = pack_weight(n((K, T)) * s)
    return {
        "x_words": packed_xT[0],
        "x_scales": packed_xT[1],
        "w1": (n((K, H)) / np.sqrt(K) / s).astype(np.float32),
        "w2": (n((K, H)) / np.sqrt(K) / s).astype(np.float32),
        "dtm": (n((H, S))).astype(np.float32),
        "unit": (np.random.uniform(0.6, 1.4, (H, 1)) * u[:, None]).astype(np.float32),
        "w3": (n((H, N)) / np.sqrt(H) / u[:, None]).astype(np.float32),
        "offs": striped(np.random.permutation(T)[:S]),
        "ft": striped(np.random.permutation(np.concatenate([np.arange(V), np.random.randint(0, V, U - V)]))),
    }


def reference(x_words, x_scales, w1, w2, dtm, unit, w3, offs, ft):
    xq = unpack_weight(x_words, x_scales)[:, unstriped(offs)]
    gy = mxq(f64(w2), 0, "e4m3").T @ xq
    yy = (gy) ** 2
    syy = yy.reshape(len(yy), -1, D).sum(axis=2) + 0.5
    gx = mxq(f64(w1), 0, "e4m3").T @ xq
    xt = gx * f64(dtm)
    sxt = xt.reshape(len(xt), -1, D).sum(axis=2)
    xy = gx * gy
    sxy = xy.reshape(len(xy), -1, D).sum(axis=2)
    yt = gy * f64(dtm)
    syt = yt.reshape(len(yt), -1, D).sum(axis=2)
    xx = (gx) ** 2
    sxx = xx.reshape(len(xx), -1, D).sum(axis=2) + 0.5
    det = sxx * syy - (0.8 * ((sxy) ** 2)) + 0.3
    u_ = (syy * sxt - (sxy * syt)) / det
    uf = u_[:, unstriped(ft)]
    hid = f64(unit) * uf
    return mxq(f64(w3), 0, "e4m3").T @ mxq(hid, 0, "e4m3")

@@ -1,0 +1,221 @@
+import math
+from contextlib import ExitStack
+
+import concourse.mybir as mybir
+from concourse.masks import make_identity
+
+K, T, S, D, N, H, V, U = 512, 4096, 1024, 4, 128, 512, 256, 512
+FLOPS = 2 * (2 * K * H * S + H * N * U)
+
+F32 = mybir.dt.float32
+BF16 = mybir.dt.bfloat16
+I32 = mybir.dt.int32
+U32 = mybir.dt.uint32
+U16 = mybir.dt.uint16
+U8 = mybir.dt.uint8
+FP8X4 = mybir.dt.float8_e4m3fn_x4
+ACT = mybir.ActivationFunctionType
+MULT = mybir.AluOpType.mult
+ADD = mybir.AluOpType.add
+
+P = 128
+PACK = 4
+HALF = 512
+LIST_COLS = 16
+
+
+def tile_picked_ylucas_flow_p_kernel(
+    tc, x_words, x_scales, w1, w2, dtm, unit, w3, offs, ft, out
+):
+    nc = tc.nc
+    with ExitStack() as ctx:
+        keep = ctx.enter_context(tc.tile_pool(name="keep", bufs=1))
+        work = ctx.enter_context(tc.tile_pool(name="work", bufs=3))
+        psum = ctx.enter_context(tc.psum_pool(name="psum", bufs=1))
+
+        offs_sb = keep.tile([P, S // LIST_COLS], U16, name="offs_sb")
+        ft_sb = keep.tile([P, U // LIST_COLS], U16, name="ft_sb")
+        xw = keep.tile([P, T], I32, name="xw")
+        xs = keep.tile([P, T], U8, name="xs")
+        w2_raw = [keep.tile([P, PACK, H // 2], F32, name=f"w2_raw{a}") for a in range(2)]
+        w1_raw = [keep.tile([P, PACK, H // 2], F32, name=f"w1_raw{a}") for a in range(2)]
+        w3_raw = keep.tile([P, PACK, N], F32, name="w3_raw")
+        dtm_sb = [keep.tile([P, S], F32, name=f"dtm{t}") for t in range(PACK)]
+        unit_sb = keep.tile([P, PACK], F32, name="unit_sb")
+        ident = keep.tile([P, P], F32, name="ident")
+        flow = [keep.tile([P, 2 * V], F32, name=f"flow{t}") for t in range(PACK)]
+
+        nc.vector.memset(xs[:].bitcast(I32), 0)
+        nc.sync.dma_start(offs_sb[:], offs)
+        nc.sync.dma_start(xw[:], x_words[0].rearrange("p c r -> p (c r)").bitcast(I32))
+        for q in range(4):
+            nc.scalar.dma_start(
+                xs[32 * q : 32 * q + 4, :].bitcast(I32), x_scales[0, 4 * q : 4 * q + 4, :].bitcast(I32)
+            )
+        for w, raw in ((w2, w2_raw), (w1, w1_raw)):
+            rows = w.rearrange("(p j) c -> p j c", j=PACK)
+            for a in range(2):
+                nc.sync.dma_start(raw[a][:], rows[:, :, a * (H // 2) : (a + 1) * (H // 2)])
+        dtm_rows = dtm.rearrange("(p t) s -> t p s", t=PACK)
+        nc.sync.dma_start(dtm_sb[0][:], dtm_rows[0])
+        nc.sync.dma_start(unit_sb[:], unit.rearrange("(p t) o -> p (t o)", t=PACK))
+        nc.sync.dma_start(ft_sb[:], ft)
+        for t in range(1, PACK):
+            nc.sync.dma_start(dtm_sb[t][:], dtm_rows[t])
+        nc.sync.dma_start(w3_raw[:], w3.rearrange("(p j) c -> p j c", j=PACK))
+
+        make_identity(nc, ident[:])
+        for t in range(PACK):
+            nc.gpsimd.memset(flow[t][:, V:], 0.0)
+
+        w2_bf = keep.tile([P, PACK, P, PACK], BF16, name="w2_bf", align_bytes=64)
+        w1_bf = keep.tile([P, PACK, P, PACK], BF16, name="w1_bf", align_bytes=64)
+        w2_codes = keep.tile([P, H], U32, name="w2_codes", align_bytes=64)
+        w1_codes = keep.tile([P, H], U32, name="w1_codes", align_bytes=64)
+        w2_sc = keep.tile([P, H], U8, name="w2_sc", align_bytes=64)
+        w1_sc = keep.tile([P, H], U8, name="w1_sc", align_bytes=64)
+
+        xg_words = [keep.tile([P, HALF], U32, name=f"xg_words{h}", align_bytes=64) for h in range(2)]
+        xg_sc = [keep.tile([P, HALF], U8, name=f"xg_sc{h}", align_bytes=64) for h in range(2)]
+
+        def gather_pixels(h):
+            picks = offs_sb[:, h * HALF // LIST_COLS : (h + 1) * HALF // LIST_COLS]
+            nc.vector.tensor_copy(xg_words[h][:], xw[:].bitcast(U32).indirect(picks))
+            nc.vector.tensor_copy(xg_sc[h][:], xs[:].indirect(picks))
+
+        def deal(copy, dst, raw, a):
+            m_half = P // 2
+            copy(
+                dst[:, :, a * m_half : (a + 1) * m_half, :].rearrange("p t m j -> p m t j"),
+                raw[a][:].rearrange("p j (m t) -> p m t j", t=PACK),
+            )
+
+        def quantise(codes, sc, bf, t0, t1):
+            flat = bf[:].rearrange("p t m j -> p (t m j)")
+            nc.vector.quantize_mx(
+                codes[:, t0 * P : t1 * P].bitcast(FP8X4), sc[:, t0 * P : t1 * P], flat[:, t0 * HALF : t1 * HALF]
+            )
+
+        gather_pixels(0)
+        gather_pixels(1)
+        deal(nc.scalar.copy, w2_bf, w2_raw, 0)
+        deal(nc.scalar.copy, w2_bf, w2_raw, 1)
+        deal(nc.scalar.copy, w1_bf, w1_raw, 0)
+        quantise(w2_codes, w2_sc, w2_bf, 0, PACK)
+        deal(nc.vector.tensor_copy, w1_bf, w1_raw, 1)
+        quantise(w1_codes, w1_sc, w1_bf, 0, 1)
+        quantise(w1_codes, w1_sc, w1_bf, 1, PACK)
+
+        w3_bf = keep.tile([P, N, PACK], BF16, name="w3_bf", align_bytes=64)
+        w3_codes = keep.tile([P, N], U32, name="w3_codes", align_bytes=64)
+        w3_sc = keep.tile([P, N], U8, name="w3_sc", align_bytes=64)
+
+        picked = [keep.tile([P, PACK, U // 2], BF16, name=f"picked{g}") for g in range(2)]
+
+        def products(t, h):
+            cols = slice(t * P, (t + 1) * P)
+            gy = psum.tile([P, HALF], F32, name="gy")
+            gx = psum.tile([P, HALF], F32, name="gx", bufs=2)
+            for acc, codes, sc in ((gy, w2_codes, w2_sc), (gx, w1_codes, w1_sc)):
+                nc.tensor.matmul_mx(
+                    acc[:], lhsT=codes[:, cols].bitcast(FP8X4), lhsT_scale=sc[:, cols],
+                    rhs=xg_words[h][:].bitcast(FP8X4), rhs_scale=xg_sc[h][:], start=True, stop=True,
+                )
+            gy_d = gy[:].rearrange("p (v d) -> p d v", d=D)
+            gx_d = gx[:].rearrange("p (v d) -> p d v", d=D)
+            y = work.tile([P, D, P], F32, name="y")
+            prods = {name: work.tile([P, D, P], F32, name=name) for name in ("yy", "xx", "xy", "yt", "xt")}
+            dt_walk = dtm_sb[t][:, h * HALF : (h + 1) * HALF].rearrange("p (b v d) -> p b d v", v=4, d=D)
+
+            def walk(tile):
+                return tile[:].rearrange("p d (b v) -> p b d v", v=4)
+
+            nc.scalar.copy(y[:], gy_d)
+            nc.vector.tensor_tensor(
+                walk(prods["xt"]), gx[:].rearrange("p (b v d) -> p b d v", v=4, d=D), dt_walk, MULT
+            )
+            nc.scalar.activation(prods["yy"][:], y[:], ACT.Square)
+            nc.vector.tensor_tensor(prods["xy"][:], gx_d, y[:], MULT)
+            last = (t, h) == (PACK - 1, 1)
+            (nc.vector if last else nc.gpsimd).tensor_tensor(walk(prods["yt"]), walk(y), dt_walk, MULT)
+            nc.scalar.activation(prods["xx"][:], gx_d, ACT.Square)
+            return prods
+
+        def add_transposed(dst, parts):
+            for n, part in enumerate(parts):
+                nc.tensor.matmul(
+                    dst, lhsT=part, rhs=ident[:], is_transpose=True, start=(n == 0), stop=(n == len(parts) - 1)
+                )
+
+        def patch_sums(prods):
+            bank_a = psum.tile([P, 2, P], F32, name="bank_a", bufs=2)
+            bank_b = psum.tile([P, 3, P], F32, name="bank_b", bufs=2)
+            sums = {
+                "xt": bank_b[:, 0], "yy": bank_a[:, 0], "xy": bank_a[:, 1], "xx": bank_b[:, 1], "yt": bank_b[:, 2],
+            }
+            for name, dst in sums.items():
+                add_transposed(dst, [prods[name][:, d, :] for d in range(D)])
+            terms = {name: work.tile([P, P], F32, name=name) for name in ("nb", "c", "q", "np", "n1", "n2")}
+            nc.scalar.activation(terms["nb"][:], sums["yy"], ACT.Copy, scale=-1.0, bias=-0.5)
+            nc.scalar.copy(terms["c"][:], sums["xy"])
+            nc.scalar.activation(terms["q"][:], sums["xy"], ACT.Square, scale=math.sqrt(0.8))
+            nc.vector.scalar_tensor_tensor(terms["np"][:], sums["xx"], 0.5, terms["nb"][:], ADD, MULT)
+            nc.vector.scalar_tensor_tensor(terms["n1"][:], sums["xt"], -1.0, terms["nb"][:], MULT, MULT)
+            nc.vector.scalar_tensor_tensor(terms["n2"][:], sums["yt"], -1.0, terms["c"][:], MULT, MULT)
+            return terms
+
+        def solve(t, h, terms):
+            back = psum.tile([P, 2, P], F32, name="back")
+            add_transposed(back[:, 0], [terms["np"][:], terms["q"][:]])
+            add_transposed(back[:, 1], [terms["n1"][:], terms["n2"][:]])
+            root = work.tile([P, P], F32, name="root")
+            inv = work.tile([P, P], F32, name="inv")
+            nc.scalar.activation(root[:], back[:, 0], ACT.Abs_reciprocal_sqrt, bias=-0.3)
+            nc.scalar.activation(inv[:], root[:], ACT.Square)
+            nc.vector.scalar_tensor_tensor(
+                flow[t][:, h * P : (h + 1) * P], back[:, 1], unit_sb[:, t : t + 1], inv[:], MULT, MULT
+            )
+
+        def fetch(t):
+            for g in range(2):
+                feats = ft_sb[:, g * LIST_COLS : (g + 1) * LIST_COLS]
+                if g == 1 and t == PACK - 1:
+                    nc.scalar.activation(picked[g][:, t, :], flow[t][:].indirect(feats), ACT.Copy)
+                else:
+                    nc.vector.tensor_copy(picked[g][:, t, :], flow[t][:].indirect(feats))
+
+        steps = [(t, h) for t in range(PACK) for h in range(2)]
+        prods, terms = {}, {}
+        for n in range(len(steps) + 2):
+            if n < len(steps):
+                prods[n] = products(*steps[n])
+            if n == 2:
+                nc.scalar.copy(
+                    w3_bf[:].rearrange("p (c i) j -> p c j i", i=4),
+                    w3_raw[:].rearrange("p j (c i) -> p c j i", i=4),
+                )
+                nc.vector.quantize_mx(w3_codes[:].bitcast(FP8X4), w3_sc[:], w3_bf[:].rearrange("p c j -> p (c j)"))
+            if n >= 2:
+                t, h = steps[n - 2]
+                solve(t, h, terms[n - 2])
+                if h == 1:
+                    fetch(t)
+            if 1 <= n <= len(steps):
+                terms[n - 1] = patch_sums(prods[n - 1])
+
+        for g in range(2):
+            hid = keep.tile([P, U // 2, PACK], BF16, name=f"hid{g}", align_bytes=64)
+            hid_codes = keep.tile([P, U // 2], U32, name=f"hid_codes{g}", align_bytes=64)
+            hid_sc = keep.tile([P, U // 2], U8, name=f"hid_sc{g}", align_bytes=64)
+            src = picked[g][:].rearrange("p t (c i) -> p c t i", i=4)
+            dst = hid[:].rearrange("p (c i) t -> p c t i", i=4)
+            nc.vector.tensor_copy(dst, src)
+            nc.vector.quantize_mx(hid_codes[:].bitcast(FP8X4), hid_sc[:], hid[:].rearrange("p r t -> p (r t)"))
+            motion = psum.tile([P, U // 2], F32, name="gx", bufs=2)
+            nc.tensor.matmul_mx(
+                motion[:], lhsT=w3_codes[:].bitcast(FP8X4), lhsT_scale=w3_sc[:],
+                rhs=hid_codes[:].bitcast(FP8X4), rhs_scale=hid_sc[:], start=True, stop=True,
+            )
+            result = keep.tile([P, U // 2], F32, name=f"result{g}")
+            nc.scalar.copy(result[:], motion[:])
+            nc.sync.dma_start(out[:, g * (U // 2) : (g + 1) * (U // 2)], result[:])

@@ -20,8 +20,11 @@ ADD = mybir.AluOpType.add
 
 P = 128
 PACK = 4
-HALF = 512
-LIST_COLS = 16
+PIXELS = 512
+PATCHES = PIXELS // D
+LIST_ROWS = 16
+LINE = 4
+FEATS = U // 2
 
 
 def tile_picked_ylucas_flow_p_kernel(
@@ -31,12 +34,12 @@ def tile_picked_ylucas_flow_p_kernel(
     with ExitStack() as ctx:
         keep = ctx.enter_context(tc.tile_pool(name="keep", bufs=1))
         work = ctx.enter_context(tc.tile_pool(name="work", bufs=3))
-        psum = ctx.enter_context(tc.psum_pool(name="psum", bufs=1))
+        psum = ctx.enter_context(tc.psum_pool(name="psum", bufs=2))
 
-        offs_sb = keep.tile([P, S // LIST_COLS], U16, name="offs_sb")
-        ft_sb = keep.tile([P, U // LIST_COLS], U16, name="ft_sb")
-        xw = keep.tile([P, T], I32, name="xw")
-        xs = keep.tile([P, T], U8, name="xs")
+        offs_sb = keep.tile([P, S // LIST_ROWS], U16, name="offs_sb")
+        ft_sb = keep.tile([P, U // LIST_ROWS], U16, name="ft_sb")
+        table_words = keep.tile([P, T], I32, name="table_words")
+        table_scales = keep.tile([P, T], U8, name="xs")
         w2_raw = [keep.tile([P, PACK, H // 2], F32, name=f"w2_raw{a}") for a in range(2)]
         w1_raw = [keep.tile([P, PACK, H // 2], F32, name=f"w1_raw{a}") for a in range(2)]
         w3_raw = keep.tile([P, PACK, N], F32, name="w3_raw")
@@ -45,177 +48,197 @@ def tile_picked_ylucas_flow_p_kernel(
         ident = keep.tile([P, P], F32, name="ident")
         flow = [keep.tile([P, 2 * V], F32, name=f"flow{t}") for t in range(PACK)]
 
-        nc.vector.memset(xs[:].bitcast(I32), 0)
+        nc.vector.memset(table_scales[:].bitcast(I32), 0)
         nc.sync.dma_start(offs_sb[:], offs)
-        nc.sync.dma_start(xw[:], x_words[0].rearrange("p c r -> p (c r)").bitcast(I32))
+        nc.sync.dma_start(table_words[:], x_words[0].rearrange("p c r -> p (c r)").bitcast(I32))
         for q in range(4):
             nc.scalar.dma_start(
-                xs[32 * q : 32 * q + 4, :].bitcast(I32), x_scales[0, 4 * q : 4 * q + 4, :].bitcast(I32)
+                table_scales[32 * q : 32 * q + 4, :].bitcast(I32), x_scales[0, 4 * q : 4 * q + 4, :].bitcast(I32)
             )
         for w, raw in ((w2, w2_raw), (w1, w1_raw)):
             rows = w.rearrange("(p j) c -> p j c", j=PACK)
             for a in range(2):
                 nc.sync.dma_start(raw[a][:], rows[:, :, a * (H // 2) : (a + 1) * (H // 2)])
-        dtm_rows = dtm.rearrange("(p t) s -> t p s", t=PACK)
-        nc.sync.dma_start(dtm_sb[0][:], dtm_rows[0])
+        dtm_planes = dtm.rearrange("(p t) s -> t p s", t=PACK)
+        nc.sync.dma_start(dtm_sb[0][:], dtm_planes[0])
         nc.sync.dma_start(unit_sb[:], unit.rearrange("(p t) o -> p (t o)", t=PACK))
         nc.sync.dma_start(ft_sb[:], ft)
         for t in range(1, PACK):
-            nc.sync.dma_start(dtm_sb[t][:], dtm_rows[t])
+            nc.sync.dma_start(dtm_sb[t][:], dtm_planes[t])
         nc.sync.dma_start(w3_raw[:], w3.rearrange("(p j) c -> p j c", j=PACK))
 
         make_identity(nc, ident[:])
         for t in range(PACK):
             nc.gpsimd.memset(flow[t][:, V:], 0.0)
+        warm = keep.tile([P, 1], F32, name="warm")
+        nc.scalar.activation(warm[:], flow[PACK - 1][:, V : V + 1], ACT.Abs_reciprocal_sqrt, bias=1.0)
+
+        def list_slice(tile, first, count):
+            return tile[:, first // LIST_ROWS : (first + count) // LIST_ROWS]
+
+        x_codes = [keep.tile([P, PIXELS], U32, name=f"x_codes{h}", align_bytes=64) for h in range(2)]
+        x_sc = [keep.tile([P, PIXELS], U8, name=f"x_sc{h}", align_bytes=64) for h in range(2)]
+
+        def gather_pixels(h):
+            picks = list_slice(offs_sb, h * PIXELS, PIXELS)
+            nc.vector.tensor_copy(x_codes[h][:], table_words[:].bitcast(U32).indirect(picks))
+            nc.vector.tensor_copy(x_sc[h][:], table_scales[:].indirect(picks))
 
         w2_bf = keep.tile([P, PACK, P, PACK], BF16, name="w2_bf", align_bytes=64)
         w1_bf = keep.tile([P, PACK, P, PACK], BF16, name="w1_bf", align_bytes=64)
+        w3_bf = keep.tile([P, N, PACK], BF16, name="w3_bf", align_bytes=64)
         w2_codes = keep.tile([P, H], U32, name="w2_codes", align_bytes=64)
         w1_codes = keep.tile([P, H], U32, name="w1_codes", align_bytes=64)
+        w3_codes = keep.tile([P, N], U32, name="w3_codes", align_bytes=64)
         w2_sc = keep.tile([P, H], U8, name="w2_sc", align_bytes=64)
         w1_sc = keep.tile([P, H], U8, name="w1_sc", align_bytes=64)
+        w3_sc = keep.tile([P, N], U8, name="w3_sc", align_bytes=64)
 
-        xg_words = [keep.tile([P, HALF], U32, name=f"xg_words{h}", align_bytes=64) for h in range(2)]
-        xg_sc = [keep.tile([P, HALF], U8, name=f"xg_sc{h}", align_bytes=64) for h in range(2)]
+        def deal(bf, raw):
+            for a, copy in enumerate((nc.scalar.copy, nc.vector.tensor_copy)):
+                copy(
+                    bf[:, :, a * (P // 2) : (a + 1) * (P // 2), :].rearrange("p t m j -> p m t j"),
+                    raw[a][:].rearrange("p j (m t) -> p m t j", t=PACK),
+                )
 
-        def gather_pixels(h):
-            picks = offs_sb[:, h * HALF // LIST_COLS : (h + 1) * HALF // LIST_COLS]
-            nc.vector.tensor_copy(xg_words[h][:], xw[:].bitcast(U32).indirect(picks))
-            nc.vector.tensor_copy(xg_sc[h][:], xs[:].indirect(picks))
-
-        def deal(copy, dst, raw, a):
-            m_half = P // 2
-            copy(
-                dst[:, :, a * m_half : (a + 1) * m_half, :].rearrange("p t m j -> p m t j"),
-                raw[a][:].rearrange("p j (m t) -> p m t j", t=PACK),
-            )
-
-        def quantise(codes, sc, bf, t0, t1):
-            flat = bf[:].rearrange("p t m j -> p (t m j)")
+        def quantise_planes(codes, sc, bf, t0, t1):
             nc.vector.quantize_mx(
-                codes[:, t0 * P : t1 * P].bitcast(FP8X4), sc[:, t0 * P : t1 * P], flat[:, t0 * HALF : t1 * HALF]
+                codes[:, t0 * P : t1 * P].bitcast(FP8X4),
+                sc[:, t0 * P : t1 * P],
+                bf[:].rearrange("p t m j -> p (t m j)")[:, t0 * P * PACK : t1 * P * PACK],
             )
 
         gather_pixels(0)
+        deal(w2_bf, w2_raw)
+        quantise_planes(w2_codes, w2_sc, w2_bf, 0, PACK)
+        deal(w1_bf, w1_raw)
+        quantise_planes(w1_codes, w1_sc, w1_bf, 0, 1)
         gather_pixels(1)
-        deal(nc.scalar.copy, w2_bf, w2_raw, 0)
-        deal(nc.scalar.copy, w2_bf, w2_raw, 1)
-        deal(nc.scalar.copy, w1_bf, w1_raw, 0)
-        quantise(w2_codes, w2_sc, w2_bf, 0, PACK)
-        deal(nc.vector.tensor_copy, w1_bf, w1_raw, 1)
-        quantise(w1_codes, w1_sc, w1_bf, 0, 1)
-        quantise(w1_codes, w1_sc, w1_bf, 1, PACK)
+        quantise_planes(w1_codes, w1_sc, w1_bf, 1, PACK)
 
-        w3_bf = keep.tile([P, N, PACK], BF16, name="w3_bf", align_bytes=64)
-        w3_codes = keep.tile([P, N], U32, name="w3_codes", align_bytes=64)
-        w3_sc = keep.tile([P, N], U8, name="w3_sc", align_bytes=64)
+        steps = [(t, h) for t in range(PACK) for h in range(2)]
+        picked = [keep.tile([P, PACK, FEATS], BF16, name=f"picked{g}") for g in range(2)]
 
-        picked = [keep.tile([P, PACK, U // 2], BF16, name=f"picked{g}") for g in range(2)]
-
-        def products(t, h):
-            cols = slice(t * P, (t + 1) * P)
-            gy = psum.tile([P, HALF], F32, name="gy")
-            gx = psum.tile([P, HALF], F32, name="gx", bufs=2)
+        def products(n):
+            t, h = steps[n]
+            channels = slice(t * P, (t + 1) * P)
+            pixels = slice(h * PIXELS, (h + 1) * PIXELS)
+            gy = psum.tile([P, PIXELS], F32, name="gy")
+            gx = psum.tile([P, PIXELS], F32, name="gx")
             for acc, codes, sc in ((gy, w2_codes, w2_sc), (gx, w1_codes, w1_sc)):
                 nc.tensor.matmul_mx(
-                    acc[:], lhsT=codes[:, cols].bitcast(FP8X4), lhsT_scale=sc[:, cols],
-                    rhs=xg_words[h][:].bitcast(FP8X4), rhs_scale=xg_sc[h][:], start=True, stop=True,
+                    acc[:], lhsT=codes[:, channels].bitcast(FP8X4), lhsT_scale=sc[:, channels],
+                    rhs=x_codes[h][:].bitcast(FP8X4), rhs_scale=x_sc[h][:], start=True, stop=True,
                 )
-            gy_d = gy[:].rearrange("p (v d) -> p d v", d=D)
-            gx_d = gx[:].rearrange("p (v d) -> p d v", d=D)
-            y = work.tile([P, D, P], F32, name="y")
-            prods = {name: work.tile([P, D, P], F32, name=name) for name in ("yy", "xx", "xy", "yt", "xt")}
-            dt_walk = dtm_sb[t][:, h * HALF : (h + 1) * HALF].rearrange("p (b v d) -> p b d v", v=4, d=D)
+            gy_by_d = gy[:].rearrange("p (v d) -> p d v", d=D)
+            gx_by_d = gx[:].rearrange("p (v d) -> p d v", d=D)
+            y = work.tile([P, D, PATCHES], F32, name="y")
+            xt = work.tile([P, PATCHES, D], F32, name="xt")
+            sxt = work.tile([P, PATCHES], F32, name="sxt")
+            prod = work.tile([P, 4, D, PATCHES], F32, name="prod")
+            xx, yt, yy, xy = (prod[:, k] for k in range(4))
 
-            def walk(tile):
-                return tile[:].rearrange("p d (b v) -> p b d v", v=4)
-
-            nc.scalar.copy(y[:], gy_d)
+            nc.scalar.copy(y[:], gy_by_d)
+            nc.vector.tensor_tensor(xt[:].rearrange("p v d -> p (v d)"), gx[:], dtm_sb[t][:, pixels], MULT)
+            nc.scalar.activation(xx, gx_by_d, ACT.Square)
             nc.vector.tensor_tensor(
-                walk(prods["xt"]), gx[:].rearrange("p (b v d) -> p b d v", v=4, d=D), dt_walk, MULT
+                yt.rearrange("p d (b v) -> p b d v", v=LINE),
+                gy[:].rearrange("p (b v d) -> p b d v", v=LINE, d=D),
+                dtm_sb[t][:, pixels].rearrange("p (b v d) -> p b d v", v=LINE, d=D),
+                MULT,
             )
-            nc.scalar.activation(prods["yy"][:], y[:], ACT.Square)
-            nc.vector.tensor_tensor(prods["xy"][:], gx_d, y[:], MULT)
-            last = (t, h) == (PACK - 1, 1)
-            (nc.vector if last else nc.gpsimd).tensor_tensor(walk(prods["yt"]), walk(y), dt_walk, MULT)
-            nc.scalar.activation(prods["xx"][:], gx_d, ACT.Square)
-            return prods
+            nc.scalar.activation(yy, gy_by_d, ACT.Square)
+            nc.vector.tensor_tensor(xy, gx_by_d, y[:], MULT)
+            nc.vector.tensor_reduce(sxt[:], xt[:], mybir.AxisListType.X, ADD)
+
+            pairs = work.tile([P, 4, 2, PATCHES], F32, name="pairs")
+            adder = nc.vector if n == len(steps) - 1 else nc.gpsimd
+            for k in (0, 2):
+                adder.tensor_tensor(
+                    pairs[:, k : k + 2].rearrange("p k e v -> p k (e v)"),
+                    prod[:, k : k + 2, 0:2].rearrange("p k e v -> p k (e v)"),
+                    prod[:, k : k + 2, 2:4].rearrange("p k e v -> p k (e v)"),
+                    ADD,
+                )
+            return sxt, pairs
 
         def add_transposed(dst, parts):
-            for n, part in enumerate(parts):
+            for e, part in enumerate(parts):
                 nc.tensor.matmul(
-                    dst, lhsT=part, rhs=ident[:], is_transpose=True, start=(n == 0), stop=(n == len(parts) - 1)
+                    dst, lhsT=part, rhs=ident[:], is_transpose=True, start=(e == 0), stop=(e == len(parts) - 1)
                 )
 
-        def patch_sums(prods):
-            bank_a = psum.tile([P, 2, P], F32, name="bank_a", bufs=2)
-            bank_b = psum.tile([P, 3, P], F32, name="bank_b", bufs=2)
-            sums = {
-                "xt": bank_b[:, 0], "yy": bank_a[:, 0], "xy": bank_a[:, 1], "xx": bank_b[:, 1], "yt": bank_b[:, 2],
-            }
-            for name, dst in sums.items():
-                add_transposed(dst, [prods[name][:, d, :] for d in range(D)])
-            terms = {name: work.tile([P, P], F32, name=name) for name in ("nb", "c", "q", "np", "n1", "n2")}
-            nc.scalar.activation(terms["nb"][:], sums["yy"], ACT.Copy, scale=-1.0, bias=-0.5)
-            nc.scalar.copy(terms["c"][:], sums["xy"])
-            nc.scalar.activation(terms["q"][:], sums["xy"], ACT.Square, scale=math.sqrt(0.8))
-            nc.vector.scalar_tensor_tensor(terms["np"][:], sums["xx"], 0.5, terms["nb"][:], ADD, MULT)
-            nc.vector.scalar_tensor_tensor(terms["n1"][:], sums["xt"], -1.0, terms["nb"][:], MULT, MULT)
-            nc.vector.scalar_tensor_tensor(terms["n2"][:], sums["yt"], -1.0, terms["c"][:], MULT, MULT)
-            return terms
+        def system_terms(sxt, pairs):
+            bank_x = psum.tile([P, 4, P], F32, name="bank_x")
+            bank_y = psum.tile([P, 3, P], F32, name="bank_y")
+            sum_xt, sum_xx, sum_yy, sum_xy = (bank_x[:, k] for k in range(4))
+            sum_yt = bank_y[:, 0]
+            add_transposed(sum_xt, [sxt[:]])
+            for k, dst in enumerate((sum_xx, sum_yt, sum_yy, sum_xy)):
+                add_transposed(dst, [pairs[:, k, 0], pairs[:, k, 1]])
+            neg_syy = work.tile([P, P], F32, name="neg_syy")
+            sxy = work.tile([P, P], F32, name="sxy")
+            terms = [work.tile([P, P], F32, name=f"term{k}") for k in range(4)]
+            nc.scalar.activation(neg_syy[:], sum_yy, ACT.Copy, scale=-1.0, bias=-0.5)
+            nc.scalar.copy(sxy[:], sum_xy)
+            nc.scalar.activation(terms[1][:], sum_xy, ACT.Square, scale=math.sqrt(0.8))
+            nc.vector.scalar_tensor_tensor(terms[0][:], sum_xx, 0.5, neg_syy[:], ADD, MULT)
+            nc.vector.scalar_tensor_tensor(terms[2][:], sum_xt, -1.0, neg_syy[:], MULT, MULT)
+            nc.vector.scalar_tensor_tensor(terms[3][:], sum_yt, -1.0, sxy[:], MULT, MULT)
+            return terms, bank_y
 
-        def solve(t, h, terms):
-            back = psum.tile([P, 2, P], F32, name="back")
-            add_transposed(back[:, 0], [terms["np"][:], terms["q"][:]])
-            add_transposed(back[:, 1], [terms["n1"][:], terms["n2"][:]])
-            root = work.tile([P, P], F32, name="root")
-            inv = work.tile([P, P], F32, name="inv")
-            nc.scalar.activation(root[:], back[:, 0], ACT.Abs_reciprocal_sqrt, bias=-0.3)
-            nc.scalar.activation(inv[:], root[:], ACT.Square)
+        def solve(n, terms, bank_y):
+            t, h = steps[n]
+            add_transposed(bank_y[:, 1], [terms[0][:], terms[1][:]])
+            add_transposed(bank_y[:, 2], [terms[2][:], terms[3][:]])
+            root = work.tile([P, PATCHES], F32, name="root")
+            inv_det = work.tile([P, PATCHES], F32, name="inv_det")
+            nc.scalar.activation(root[:], bank_y[:, 1], ACT.Abs_reciprocal_sqrt, bias=-0.3)
+            nc.scalar.activation(inv_det[:], root[:], ACT.Square)
             nc.vector.scalar_tensor_tensor(
-                flow[t][:, h * P : (h + 1) * P], back[:, 1], unit_sb[:, t : t + 1], inv[:], MULT, MULT
+                flow[t][:, h * PATCHES : (h + 1) * PATCHES], bank_y[:, 2], unit_sb[:, t : t + 1], inv_det[:],
+                MULT, MULT,
             )
 
         def fetch(t):
             for g in range(2):
-                feats = ft_sb[:, g * LIST_COLS : (g + 1) * LIST_COLS]
-                if g == 1 and t == PACK - 1:
-                    nc.scalar.activation(picked[g][:, t, :], flow[t][:].indirect(feats), ACT.Copy)
+                window = flow[t][:].indirect(list_slice(ft_sb, g * FEATS, FEATS))
+                if t == PACK - 1 and g == 0:
+                    nc.vector.tensor_copy(picked[g][:, t, :], window)
                 else:
-                    nc.vector.tensor_copy(picked[g][:, t, :], flow[t][:].indirect(feats))
+                    nc.scalar.activation(picked[g][:, t, :], window, ACT.Copy)
 
-        steps = [(t, h) for t in range(PACK) for h in range(2)]
-        prods, terms = {}, {}
+        partial, system = {}, {}
         for n in range(len(steps) + 2):
             if n < len(steps):
-                prods[n] = products(*steps[n])
+                partial[n] = products(n)
             if n == 2:
                 nc.scalar.copy(
-                    w3_bf[:].rearrange("p (c i) j -> p c j i", i=4),
-                    w3_raw[:].rearrange("p j (c i) -> p c j i", i=4),
+                    w3_bf[:].rearrange("p (c i) j -> p c j i", i=LINE),
+                    w3_raw[:].rearrange("p j (c i) -> p c j i", i=LINE),
                 )
                 nc.vector.quantize_mx(w3_codes[:].bitcast(FP8X4), w3_sc[:], w3_bf[:].rearrange("p c j -> p (c j)"))
             if n >= 2:
-                t, h = steps[n - 2]
-                solve(t, h, terms[n - 2])
-                if h == 1:
-                    fetch(t)
+                solve(n - 2, *system[n - 2])
+                if steps[n - 2][1] == 1:
+                    fetch(steps[n - 2][0])
             if 1 <= n <= len(steps):
-                terms[n - 1] = patch_sums(prods[n - 1])
+                system[n - 1] = system_terms(*partial[n - 1])
 
         for g in range(2):
-            hid = keep.tile([P, U // 2, PACK], BF16, name=f"hid{g}", align_bytes=64)
-            hid_codes = keep.tile([P, U // 2], U32, name=f"hid_codes{g}", align_bytes=64)
-            hid_sc = keep.tile([P, U // 2], U8, name=f"hid_sc{g}", align_bytes=64)
-            src = picked[g][:].rearrange("p t (c i) -> p c t i", i=4)
-            dst = hid[:].rearrange("p (c i) t -> p c t i", i=4)
-            nc.vector.tensor_copy(dst, src)
+            hid = keep.tile([P, FEATS, PACK], BF16, name=f"hid{g}", align_bytes=64)
+            hid_codes = keep.tile([P, FEATS], U32, name=f"hid_codes{g}", align_bytes=64)
+            hid_sc = keep.tile([P, FEATS], U8, name=f"hid_sc{g}", align_bytes=64)
+            nc.vector.tensor_copy(
+                hid[:].rearrange("p (c i) t -> p c t i", i=LINE),
+                picked[g][:].rearrange("p t (c i) -> p c t i", i=LINE),
+            )
             nc.vector.quantize_mx(hid_codes[:].bitcast(FP8X4), hid_sc[:], hid[:].rearrange("p r t -> p (r t)"))
-            motion = psum.tile([P, U // 2], F32, name="gx", bufs=2)
+            motion = psum.tile([P, FEATS], F32, name="gx")
             nc.tensor.matmul_mx(
                 motion[:], lhsT=w3_codes[:].bitcast(FP8X4), lhsT_scale=w3_sc[:],
                 rhs=hid_codes[:].bitcast(FP8X4), rhs_scale=hid_sc[:], start=True, stop=True,
             )
-            result = keep.tile([P, U // 2], F32, name=f"result{g}")
+            result = keep.tile([P, FEATS], F32, name=f"result{g}")
             nc.scalar.copy(result[:], motion[:])
-            nc.sync.dma_start(out[:, g * (U // 2) : (g + 1) * (U // 2)], result[:])
+            nc.sync.dma_start(out[:, g * FEATS : (g + 1) * FEATS], result[:])

@@ -94,12 +94,11 @@ def tile_picked_ylucas_flow_p_kernel(
         w1_sc = keep.tile([P, H], U8, name="w1_sc", align_bytes=64)
         w3_sc = keep.tile([P, N], U8, name="w3_sc", align_bytes=64)
 
-        def deal(bf, raw):
-            for a, copy in enumerate((nc.scalar.copy, nc.vector.tensor_copy)):
-                copy(
-                    bf[:, :, a * (P // 2) : (a + 1) * (P // 2), :].rearrange("p t m j -> p m t j"),
-                    raw[a][:].rearrange("p j (m t) -> p m t j", t=PACK),
-                )
+        def deal(copy, bf, raw, a):
+            copy(
+                bf[:, :, a * (P // 2) : (a + 1) * (P // 2), :].rearrange("p t m j -> p m t j"),
+                raw[a][:].rearrange("p j (m t) -> p m t j", t=PACK),
+            )
 
         def quantise_planes(codes, sc, bf, t0, t1):
             nc.vector.quantize_mx(
@@ -109,11 +108,13 @@ def tile_picked_ylucas_flow_p_kernel(
             )
 
         gather_pixels(0)
-        deal(w2_bf, w2_raw)
-        quantise_planes(w2_codes, w2_sc, w2_bf, 0, PACK)
-        deal(w1_bf, w1_raw)
-        quantise_planes(w1_codes, w1_sc, w1_bf, 0, 1)
         gather_pixels(1)
+        deal(nc.scalar.copy, w2_bf, w2_raw, 0)
+        deal(nc.scalar.copy, w2_bf, w2_raw, 1)
+        deal(nc.scalar.copy, w1_bf, w1_raw, 0)
+        quantise_planes(w2_codes, w2_sc, w2_bf, 0, PACK)
+        deal(nc.vector.tensor_copy, w1_bf, w1_raw, 1)
+        quantise_planes(w1_codes, w1_sc, w1_bf, 0, 1)
         quantise_planes(w1_codes, w1_sc, w1_bf, 1, PACK)
 
         steps = [(t, h) for t in range(PACK) for h in range(2)]
@@ -135,32 +136,30 @@ def tile_picked_ylucas_flow_p_kernel(
             y = work.tile([P, D, PATCHES], F32, name="y")
             xt = work.tile([P, PATCHES, D], F32, name="xt")
             sxt = work.tile([P, PATCHES], F32, name="sxt")
-            prod = work.tile([P, 4, D, PATCHES], F32, name="prod")
-            xx, yt, yy, xy = (prod[:, k] for k in range(4))
+            by_d = work.tile([P, 2, D, PATCHES], F32, name="by_d")
+            by_v = work.tile([P, 2, PATCHES, D], F32, name="by_v")
+            dt = dtm_sb[t][:, pixels]
 
             nc.scalar.copy(y[:], gy_by_d)
-            nc.vector.tensor_tensor(xt[:].rearrange("p v d -> p (v d)"), gx[:], dtm_sb[t][:, pixels], MULT)
-            nc.scalar.activation(xx, gx_by_d, ACT.Square)
-            nc.vector.tensor_tensor(
-                yt.rearrange("p d (b v) -> p b d v", v=LINE),
-                gy[:].rearrange("p (b v d) -> p b d v", v=LINE, d=D),
-                dtm_sb[t][:, pixels].rearrange("p (b v d) -> p b d v", v=LINE, d=D),
-                MULT,
-            )
-            nc.scalar.activation(yy, gy_by_d, ACT.Square)
-            nc.vector.tensor_tensor(xy, gx_by_d, y[:], MULT)
+            nc.vector.tensor_tensor(xt[:].rearrange("p v d -> p (v d)"), gx[:], dt, MULT)
+            nc.scalar.activation(by_d[:, 0], gy_by_d, ACT.Square)
+            nc.vector.tensor_tensor(by_d[:, 1], gx_by_d, y[:], MULT)
+            nc.scalar.activation(by_v[:, 0].rearrange("p v d -> p (v d)"), gx[:], ACT.Square)
+            nc.vector.tensor_tensor(by_v[:, 1].rearrange("p v d -> p (v d)"), gy[:], dt, MULT)
             nc.vector.tensor_reduce(sxt[:], xt[:], mybir.AxisListType.X, ADD)
 
-            pairs = work.tile([P, 4, 2, PATCHES], F32, name="pairs")
+            pairs_d = work.tile([P, 2, 2, PATCHES], F32, name="pairs_d")
+            pairs_v = work.tile([P, 2, PATCHES, 2], F32, name="pairs_v")
             adder = nc.vector if n == len(steps) - 1 else nc.gpsimd
-            for k in (0, 2):
-                adder.tensor_tensor(
-                    pairs[:, k : k + 2].rearrange("p k e v -> p k (e v)"),
-                    prod[:, k : k + 2, 0:2].rearrange("p k e v -> p k (e v)"),
-                    prod[:, k : k + 2, 2:4].rearrange("p k e v -> p k (e v)"),
-                    ADD,
-                )
-            return sxt, pairs
+            adder.tensor_tensor(pairs_d[:], by_d[:, :, 0:2], by_d[:, :, 2:4], ADD)
+            adder.tensor_tensor(pairs_v[:], by_v[:, :, :, 0:2], by_v[:, :, :, 2:4], ADD)
+            return {
+                "xt": [sxt[:]],
+                "yy": [pairs_d[:, 0, e] for e in range(2)],
+                "xy": [pairs_d[:, 1, e] for e in range(2)],
+                "xx": [pairs_v[:, 0, :, e] for e in range(2)],
+                "yt": [pairs_v[:, 1, :, e] for e in range(2)],
+            }
 
         def add_transposed(dst, parts):
             for e, part in enumerate(parts):
@@ -168,14 +167,13 @@ def tile_picked_ylucas_flow_p_kernel(
                     dst, lhsT=part, rhs=ident[:], is_transpose=True, start=(e == 0), stop=(e == len(parts) - 1)
                 )
 
-        def system_terms(sxt, pairs):
-            bank_x = psum.tile([P, 4, P], F32, name="bank_x")
-            bank_y = psum.tile([P, 3, P], F32, name="bank_y")
-            sum_xt, sum_xx, sum_yy, sum_xy = (bank_x[:, k] for k in range(4))
-            sum_yt = bank_y[:, 0]
-            add_transposed(sum_xt, [sxt[:]])
-            for k, dst in enumerate((sum_xx, sum_yt, sum_yy, sum_xy)):
-                add_transposed(dst, [pairs[:, k, 0], pairs[:, k, 1]])
+        def system_terms(parts):
+            bank_x = psum.tile([P, 3, P], F32, name="bank_x")
+            bank_y = psum.tile([P, 4, P], F32, name="bank_y")
+            sum_yy, sum_xy = bank_x[:, 0], bank_x[:, 1]
+            sum_xt, sum_xx, sum_yt = bank_y[:, 0], bank_y[:, 1], bank_y[:, 2]
+            for name, dst in (("xt", sum_xt), ("yy", sum_yy), ("xy", sum_xy), ("xx", sum_xx), ("yt", sum_yt)):
+                add_transposed(dst, parts[name])
             neg_syy = work.tile([P, P], F32, name="neg_syy")
             sxy = work.tile([P, P], F32, name="sxy")
             terms = [work.tile([P, P], F32, name=f"term{k}") for k in range(4)]
@@ -185,25 +183,25 @@ def tile_picked_ylucas_flow_p_kernel(
             nc.vector.scalar_tensor_tensor(terms[0][:], sum_xx, 0.5, neg_syy[:], ADD, MULT)
             nc.vector.scalar_tensor_tensor(terms[2][:], sum_xt, -1.0, neg_syy[:], MULT, MULT)
             nc.vector.scalar_tensor_tensor(terms[3][:], sum_yt, -1.0, sxy[:], MULT, MULT)
-            return terms, bank_y
+            return terms, bank_x[:, 2], bank_y[:, 3]
 
-        def solve(n, terms, bank_y):
+        def solve(n, terms, neg_det, num):
             t, h = steps[n]
-            add_transposed(bank_y[:, 1], [terms[0][:], terms[1][:]])
-            add_transposed(bank_y[:, 2], [terms[2][:], terms[3][:]])
+            add_transposed(neg_det, [terms[0][:], terms[1][:]])
+            add_transposed(num, [terms[2][:], terms[3][:]])
             root = work.tile([P, PATCHES], F32, name="root")
             inv_det = work.tile([P, PATCHES], F32, name="inv_det")
-            nc.scalar.activation(root[:], bank_y[:, 1], ACT.Abs_reciprocal_sqrt, bias=-0.3)
+            nc.scalar.activation(root[:], neg_det, ACT.Abs_reciprocal_sqrt, bias=-0.3)
             nc.scalar.activation(inv_det[:], root[:], ACT.Square)
             nc.vector.scalar_tensor_tensor(
-                flow[t][:, h * PATCHES : (h + 1) * PATCHES], bank_y[:, 2], unit_sb[:, t : t + 1], inv_det[:],
+                flow[t][:, h * PATCHES : (h + 1) * PATCHES], num, unit_sb[:, t : t + 1], inv_det[:],
                 MULT, MULT,
             )
 
         def fetch(t):
             for g in range(2):
                 window = flow[t][:].indirect(list_slice(ft_sb, g * FEATS, FEATS))
-                if t == PACK - 1 and g == 0:
+                if t >= PACK - 2 and g == 0:
                     nc.vector.tensor_copy(picked[g][:, t, :], window)
                 else:
                     nc.scalar.activation(picked[g][:, t, :], window, ACT.Copy)
@@ -223,7 +221,7 @@ def tile_picked_ylucas_flow_p_kernel(
                 if steps[n - 2][1] == 1:
                     fetch(steps[n - 2][0])
             if 1 <= n <= len(steps):
-                system[n - 1] = system_terms(*partial[n - 1])
+                system[n - 1] = system_terms(partial[n - 1])
 
         for g in range(2):
             hid = keep.tile([P, FEATS, PACK], BF16, name=f"hid{g}", align_bytes=64)

@@ -137,28 +137,33 @@ def tile_picked_ylucas_flow_p_kernel(
             xt = work.tile([P, PATCHES, D], F32, name="xt")
             sxt = work.tile([P, PATCHES], F32, name="sxt")
             by_d = work.tile([P, 2, D, PATCHES], F32, name="by_d")
-            by_v = work.tile([P, 2, PATCHES, D], F32, name="by_v")
+            by_e = work.tile([P, 2, 2, PATCHES, 2], F32, name="by_e")
             dt = dtm_sb[t][:, pixels]
 
             nc.scalar.copy(y[:], gy_by_d)
             nc.vector.tensor_tensor(xt[:].rearrange("p v d -> p (v d)"), gx[:], dt, MULT)
             nc.scalar.activation(by_d[:, 0], gy_by_d, ACT.Square)
             nc.vector.tensor_tensor(by_d[:, 1], gx_by_d, y[:], MULT)
-            nc.scalar.activation(by_v[:, 0].rearrange("p v d -> p (v d)"), gx[:], ACT.Square)
-            nc.vector.tensor_tensor(by_v[:, 1].rearrange("p v d -> p (v d)"), gy[:], dt, MULT)
+            nc.scalar.activation(by_e[:, 0], gx[:].rearrange("p (v e f) -> p e v f", e=2, f=2), ACT.Square)
+            nc.vector.tensor_tensor(
+                by_e[:, 1].rearrange("p e v f -> p v e f"),
+                gy[:].rearrange("p (v e f) -> p v e f", e=2, f=2),
+                dt.rearrange("p (v e f) -> p v e f", e=2, f=2),
+                MULT,
+            )
             nc.vector.tensor_reduce(sxt[:], xt[:], mybir.AxisListType.X, ADD)
 
             pairs_d = work.tile([P, 2, 2, PATCHES], F32, name="pairs_d")
-            pairs_v = work.tile([P, 2, PATCHES, 2], F32, name="pairs_v")
+            pairs_e = work.tile([P, 2, 2, PATCHES], F32, name="pairs_e")
             adder = nc.vector if n == len(steps) - 1 else nc.gpsimd
             adder.tensor_tensor(pairs_d[:], by_d[:, :, 0:2], by_d[:, :, 2:4], ADD)
-            adder.tensor_tensor(pairs_v[:], by_v[:, :, :, 0:2], by_v[:, :, :, 2:4], ADD)
+            adder.tensor_tensor(pairs_e[:], by_e[:, :, :, :, 0], by_e[:, :, :, :, 1], ADD)
             return {
                 "xt": [sxt[:]],
                 "yy": [pairs_d[:, 0, e] for e in range(2)],
                 "xy": [pairs_d[:, 1, e] for e in range(2)],
-                "xx": [pairs_v[:, 0, :, e] for e in range(2)],
-                "yt": [pairs_v[:, 1, :, e] for e in range(2)],
+                "xx": [pairs_e[:, 0, e] for e in range(2)],
+                "yt": [pairs_e[:, 1, e] for e in range(2)],
             }
 
         def add_transposed(dst, parts):
@@ -168,8 +173,8 @@ def tile_picked_ylucas_flow_p_kernel(
                 )
 
         def system_terms(parts):
-            bank_x = psum.tile([P, 3, P], F32, name="bank_x")
-            bank_y = psum.tile([P, 4, P], F32, name="bank_y")
+            bank_x = psum.tile([P, 2, P], F32, name="bank_x", bufs=1)
+            bank_y = psum.tile([P, 3, P], F32, name="bank_y", bufs=1)
             sum_yy, sum_xy = bank_x[:, 0], bank_x[:, 1]
             sum_xt, sum_xx, sum_yt = bank_y[:, 0], bank_y[:, 1], bank_y[:, 2]
             for name, dst in (("xt", sum_xt), ("yy", sum_yy), ("xy", sum_xy), ("xx", sum_xx), ("yt", sum_yt)):
@@ -183,10 +188,13 @@ def tile_picked_ylucas_flow_p_kernel(
             nc.vector.scalar_tensor_tensor(terms[0][:], sum_xx, 0.5, neg_syy[:], ADD, MULT)
             nc.vector.scalar_tensor_tensor(terms[2][:], sum_xt, -1.0, neg_syy[:], MULT, MULT)
             nc.vector.scalar_tensor_tensor(terms[3][:], sum_yt, -1.0, sxy[:], MULT, MULT)
-            return terms, bank_x[:, 2], bank_y[:, 3]
+            return terms
 
-        def solve(n, terms, neg_det, num):
+        def solve(n, terms):
             t, h = steps[n]
+            det_bank = psum.tile([P, P], F32, name="det_bank", bufs=1)
+            num_bank = psum.tile([P, P], F32, name="num_bank", bufs=1)
+            neg_det, num = det_bank[:], num_bank[:]
             add_transposed(neg_det, [terms[0][:], terms[1][:]])
             add_transposed(num, [terms[2][:], terms[3][:]])
             root = work.tile([P, PATCHES], F32, name="root")
@@ -217,7 +225,7 @@ def tile_picked_ylucas_flow_p_kernel(
                 )
                 nc.vector.quantize_mx(w3_codes[:].bitcast(FP8X4), w3_sc[:], w3_bf[:].rearrange("p c j -> p (c j)"))
             if n >= 2:
-                solve(n - 2, *system[n - 2])
+                solve(n - 2, system[n - 2])
                 if steps[n - 2][1] == 1:
                     fetch(steps[n - 2][0])
             if 1 <= n <= len(steps):

import math
from contextlib import ExitStack

import concourse.mybir as mybir
from concourse.masks import make_identity

K, T, S, D, N, H, V, U = 512, 4096, 1024, 4, 128, 512, 256, 512
FLOPS = 2 * (2 * K * H * S + H * N * U)

F32 = mybir.dt.float32
BF16 = mybir.dt.bfloat16
I32 = mybir.dt.int32
U32 = mybir.dt.uint32
U16 = mybir.dt.uint16
U8 = mybir.dt.uint8
FP8X4 = mybir.dt.float8_e4m3fn_x4
ACT = mybir.ActivationFunctionType
MULT = mybir.AluOpType.mult
ADD = mybir.AluOpType.add

P = 128
PACK = 4
PIXELS = 512
PATCHES = PIXELS // D
LIST_ROWS = 16
LINE = 4
FEATS = U // 2


def tile_picked_ylucas_flow_p_kernel(
    tc, x_words, x_scales, w1, w2, dtm, unit, w3, offs, ft, out
):
    nc = tc.nc
    with ExitStack() as ctx:
        keep = ctx.enter_context(tc.tile_pool(name="keep", bufs=1))
        work = ctx.enter_context(tc.tile_pool(name="work", bufs=3))
        psum = ctx.enter_context(tc.psum_pool(name="psum", bufs=2))

        offs_sb = keep.tile([P, S // LIST_ROWS], U16, name="offs_sb")
        ft_sb = keep.tile([P, U // LIST_ROWS], U16, name="ft_sb")
        table_words = keep.tile([P, T], I32, name="table_words")
        table_scales = keep.tile([P, T], U8, name="xs")
        w2_raw = [keep.tile([P, PACK, H // 2], F32, name=f"w2_raw{a}") for a in range(2)]
        w1_raw = [keep.tile([P, PACK, H // 2], F32, name=f"w1_raw{a}") for a in range(2)]
        w3_raw = keep.tile([P, PACK, N], F32, name="w3_raw")
        dtm_sb = [keep.tile([P, S], F32, name=f"dtm{t}") for t in range(PACK)]
        unit_sb = keep.tile([P, PACK], F32, name="unit_sb")
        ident = keep.tile([P, P], F32, name="ident")
        flow = [keep.tile([P, 2 * V], F32, name=f"flow{t}") for t in range(PACK)]

        nc.vector.memset(table_scales[:].bitcast(I32), 0)
        nc.sync.dma_start(offs_sb[:], offs)
        nc.sync.dma_start(table_words[:], x_words[0].rearrange("p c r -> p (c r)").bitcast(I32))
        for q in range(4):
            nc.scalar.dma_start(
                table_scales[32 * q : 32 * q + 4, :].bitcast(I32), x_scales[0, 4 * q : 4 * q + 4, :].bitcast(I32)
            )
        for w, raw in ((w2, w2_raw), (w1, w1_raw)):
            rows = w.rearrange("(p j) c -> p j c", j=PACK)
            for a in range(2):
                nc.sync.dma_start(raw[a][:], rows[:, :, a * (H // 2) : (a + 1) * (H // 2)])
        dtm_planes = dtm.rearrange("(p t) s -> t p s", t=PACK)
        nc.sync.dma_start(dtm_sb[0][:], dtm_planes[0])
        nc.sync.dma_start(unit_sb[:], unit.rearrange("(p t) o -> p (t o)", t=PACK))
        nc.sync.dma_start(ft_sb[:], ft)
        for t in range(1, PACK):
            nc.sync.dma_start(dtm_sb[t][:], dtm_planes[t])
        nc.sync.dma_start(w3_raw[:], w3.rearrange("(p j) c -> p j c", j=PACK))

        make_identity(nc, ident[:])
        for t in range(PACK):
            nc.gpsimd.memset(flow[t][:, V:], 0.0)
        warm = keep.tile([P, 1], F32, name="warm")
        nc.scalar.activation(warm[:], flow[PACK - 1][:, V : V + 1], ACT.Abs_reciprocal_sqrt, bias=1.0)

        def list_slice(tile, first, count):
            return tile[:, first // LIST_ROWS : (first + count) // LIST_ROWS]

        x_codes = [keep.tile([P, PIXELS], U32, name=f"x_codes{h}", align_bytes=64) for h in range(2)]
        x_sc = [keep.tile([P, PIXELS], U8, name=f"x_sc{h}", align_bytes=64) for h in range(2)]

        def gather_pixels(h):
            picks = list_slice(offs_sb, h * PIXELS, PIXELS)
            nc.vector.tensor_copy(x_codes[h][:], table_words[:].bitcast(U32).indirect(picks))
            nc.vector.tensor_copy(x_sc[h][:], table_scales[:].indirect(picks))

        w2_bf = keep.tile([P, PACK, P, PACK], BF16, name="w2_bf", align_bytes=64)
        w1_bf = keep.tile([P, PACK, P, PACK], BF16, name="w1_bf", align_bytes=64)
        w3_bf = keep.tile([P, N, PACK], BF16, name="w3_bf", align_bytes=64)
        w2_codes = keep.tile([P, H], U32, name="w2_codes", align_bytes=64)
        w1_codes = keep.tile([P, H], U32, name="w1_codes", align_bytes=64)
        w3_codes = keep.tile([P, N], U32, name="w3_codes", align_bytes=64)
        w2_sc = keep.tile([P, H], U8, name="w2_sc", align_bytes=64)
        w1_sc = keep.tile([P, H], U8, name="w1_sc", align_bytes=64)
        w3_sc = keep.tile([P, N], U8, name="w3_sc", align_bytes=64)

        def deal(copy, bf, raw, a):
            copy(
                bf[:, :, a * (P // 2) : (a + 1) * (P // 2), :].rearrange("p t m j -> p m t j"),
                raw[a][:].rearrange("p j (m t) -> p m t j", t=PACK),
            )

        def quantise_planes(codes, sc, bf, t0, t1):
            nc.vector.quantize_mx(
                codes[:, t0 * P : t1 * P].bitcast(FP8X4),
                sc[:, t0 * P : t1 * P],
                bf[:].rearrange("p t m j -> p (t m j)")[:, t0 * P * PACK : t1 * P * PACK],
            )

        gather_pixels(0)
        gather_pixels(1)
        deal(nc.scalar.copy, w2_bf, w2_raw, 0)
        deal(nc.scalar.copy, w2_bf, w2_raw, 1)
        deal(nc.scalar.copy, w1_bf, w1_raw, 0)
        quantise_planes(w2_codes, w2_sc, w2_bf, 0, PACK)
        deal(nc.vector.tensor_copy, w1_bf, w1_raw, 1)
        quantise_planes(w1_codes, w1_sc, w1_bf, 0, 1)
        quantise_planes(w1_codes, w1_sc, w1_bf, 1, PACK)

        steps = [(t, h) for t in range(PACK) for h in range(2)]
        picked = [keep.tile([P, PACK, FEATS], BF16, name=f"picked{g}") for g in range(2)]

        def products(n):
            t, h = steps[n]
            channels = slice(t * P, (t + 1) * P)
            pixels = slice(h * PIXELS, (h + 1) * PIXELS)
            gy = psum.tile([P, PIXELS], F32, name="gy")
            gx = psum.tile([P, PIXELS], F32, name="gx")
            for acc, codes, sc in ((gy, w2_codes, w2_sc), (gx, w1_codes, w1_sc)):
                nc.tensor.matmul_mx(
                    acc[:], lhsT=codes[:, channels].bitcast(FP8X4), lhsT_scale=sc[:, channels],
                    rhs=x_codes[h][:].bitcast(FP8X4), rhs_scale=x_sc[h][:], start=True, stop=True,
                )
            gy_by_d = gy[:].rearrange("p (v d) -> p d v", d=D)
            gx_by_d = gx[:].rearrange("p (v d) -> p d v", d=D)
            y = work.tile([P, D, PATCHES], F32, name="y")
            xt = work.tile([P, PATCHES, D], F32, name="xt")
            sxt = work.tile([P, PATCHES], F32, name="sxt")
            by_d = work.tile([P, 2, D, PATCHES], F32, name="by_d")
            by_e = work.tile([P, 2, 2, PATCHES, 2], F32, name="by_e")
            dt = dtm_sb[t][:, pixels]

            nc.scalar.copy(y[:], gy_by_d)
            nc.vector.tensor_tensor(xt[:].rearrange("p v d -> p (v d)"), gx[:], dt, MULT)
            nc.scalar.activation(by_d[:, 0], gy_by_d, ACT.Square)
            nc.vector.tensor_tensor(by_d[:, 1], gx_by_d, y[:], MULT)
            nc.scalar.activation(by_e[:, 0], gx[:].rearrange("p (v e f) -> p e v f", e=2, f=2), ACT.Square)
            nc.vector.tensor_tensor(
                by_e[:, 1].rearrange("p e v f -> p v e f"),
                gy[:].rearrange("p (v e f) -> p v e f", e=2, f=2),
                dt.rearrange("p (v e f) -> p v e f", e=2, f=2),
                MULT,
            )
            nc.vector.tensor_reduce(sxt[:], xt[:], mybir.AxisListType.X, ADD)

            pairs_d = work.tile([P, 2, 2, PATCHES], F32, name="pairs_d")
            pairs_e = work.tile([P, 2, 2, PATCHES], F32, name="pairs_e")
            adder = nc.vector if n == len(steps) - 1 else nc.gpsimd
            adder.tensor_tensor(pairs_d[:], by_d[:, :, 0:2], by_d[:, :, 2:4], ADD)
            adder.tensor_tensor(pairs_e[:], by_e[:, :, :, :, 0], by_e[:, :, :, :, 1], ADD)
            return {
                "xt": [sxt[:]],
                "yy": [pairs_d[:, 0, e] for e in range(2)],
                "xy": [pairs_d[:, 1, e] for e in range(2)],
                "xx": [pairs_e[:, 0, e] for e in range(2)],
                "yt": [pairs_e[:, 1, e] for e in range(2)],
            }

        def add_transposed(dst, parts):
            for e, part in enumerate(parts):
                nc.tensor.matmul(
                    dst, lhsT=part, rhs=ident[:], is_transpose=True, start=(e == 0), stop=(e == len(parts) - 1)
                )

        def system_terms(parts):
            bank_x = psum.tile([P, 2, P], F32, name="bank_x", bufs=1)
            bank_y = psum.tile([P, 3, P], F32, name="bank_y", bufs=1)
            sum_yy, sum_xy = bank_x[:, 0], bank_x[:, 1]
            sum_xt, sum_xx, sum_yt = bank_y[:, 0], bank_y[:, 1], bank_y[:, 2]
            for name, dst in (("xt", sum_xt), ("yy", sum_yy), ("xy", sum_xy), ("xx", sum_xx), ("yt", sum_yt)):
                add_transposed(dst, parts[name])
            neg_syy = work.tile([P, P], F32, name="neg_syy")
            sxy = work.tile([P, P], F32, name="sxy")
            terms = [work.tile([P, P], F32, name=f"term{k}") for k in range(4)]
            nc.scalar.activation(neg_syy[:], sum_yy, ACT.Copy, scale=-1.0, bias=-0.5)
            nc.scalar.copy(sxy[:], sum_xy)
            nc.scalar.activation(terms[1][:], sum_xy, ACT.Square, scale=math.sqrt(0.8))
            nc.vector.scalar_tensor_tensor(terms[0][:], sum_xx, 0.5, neg_syy[:], ADD, MULT)
            nc.vector.scalar_tensor_tensor(terms[2][:], sum_xt, -1.0, neg_syy[:], MULT, MULT)
            nc.vector.scalar_tensor_tensor(terms[3][:], sum_yt, -1.0, sxy[:], MULT, MULT)
            return terms

        def solve(n, terms):
            t, h = steps[n]
            det_bank = psum.tile([P, P], F32, name="det_bank", bufs=1)
            num_bank = psum.tile([P, P], F32, name="num_bank", bufs=1)
            neg_det, num = det_bank[:], num_bank[:]
            add_transposed(neg_det, [terms[0][:], terms[1][:]])
            add_transposed(num, [terms[2][:], terms[3][:]])
            root = work.tile([P, PATCHES], F32, name="root")
            inv_det = work.tile([P, PATCHES], F32, name="inv_det")
            nc.scalar.activation(root[:], neg_det, ACT.Abs_reciprocal_sqrt, bias=-0.3)
            nc.scalar.activation(inv_det[:], root[:], ACT.Square)
            nc.vector.scalar_tensor_tensor(
                flow[t][:, h * PATCHES : (h + 1) * PATCHES], num, unit_sb[:, t : t + 1], inv_det[:],
                MULT, MULT,
            )

        def fetch(t):
            for g in range(2):
                window = flow[t][:].indirect(list_slice(ft_sb, g * FEATS, FEATS))
                if t >= PACK - 2 and g == 0:
                    nc.vector.tensor_copy(picked[g][:, t, :], window)
                else:
                    nc.scalar.activation(picked[g][:, t, :], window, ACT.Copy)

        partial, system = {}, {}
        for n in range(len(steps) + 2):
            if n < len(steps):
                partial[n] = products(n)
            if n == 2:
                nc.scalar.copy(
                    w3_bf[:].rearrange("p (c i) j -> p c j i", i=LINE),
                    w3_raw[:].rearrange("p j (c i) -> p c j i", i=LINE),
                )
                nc.vector.quantize_mx(w3_codes[:].bitcast(FP8X4), w3_sc[:], w3_bf[:].rearrange("p c j -> p (c j)"))
            if n >= 2:
                solve(n - 2, system[n - 2])
                if steps[n - 2][1] == 1:
                    fetch(steps[n - 2][0])
            if 1 <= n <= len(steps):
                system[n - 1] = system_terms(partial[n - 1])

        for g in range(2):
            hid = keep.tile([P, FEATS, PACK], BF16, name=f"hid{g}", align_bytes=64)
            hid_codes = keep.tile([P, FEATS], U32, name=f"hid_codes{g}", align_bytes=64)
            hid_sc = keep.tile([P, FEATS], U8, name=f"hid_sc{g}", align_bytes=64)
            nc.vector.tensor_copy(
                hid[:].rearrange("p (c i) t -> p c t i", i=LINE),
                picked[g][:].rearrange("p t (c i) -> p c t i", i=LINE),
            )
            nc.vector.quantize_mx(hid_codes[:].bitcast(FP8X4), hid_sc[:], hid[:].rearrange("p r t -> p (r t)"))
            motion = psum.tile([P, FEATS], F32, name="gx")
            nc.tensor.matmul_mx(
                motion[:], lhsT=w3_codes[:].bitcast(FP8X4), lhsT_scale=w3_sc[:],
                rhs=hid_codes[:].bitcast(FP8X4), rhs_scale=hid_sc[:], start=True, stop=True,
            )
            result = keep.tile([P, FEATS], F32, name=f"result{g}")
            nc.scalar.copy(result[:], motion[:])
            nc.sync.dma_start(out[:, g * FEATS : (g + 1) * FEATS], result[:])
